import numpy as np
import ml_dtypes


def mxq(x, axis, fmt="e4m3"):
    dtype, down = {"e4m3": (ml_dtypes.float8_e4m3fn, 7), "e5m2": (ml_dtypes.float8_e5m2, 14)}[fmt]
    v = np.moveaxis(np.asarray(x, np.float32).astype(ml_dtypes.bfloat16).astype(np.float64), axis, -1)
    blocks = v.reshape(v.shape[:-1] + (-1, 32))
    amax = np.abs(blocks).max(-1, keepdims=True)
    byte = np.maximum(np.where(amax > 0, np.frexp(amax)[1] - 1 + 127, 0) - down, 1)
    scale = np.exp2(byte - 127.0)
    codes = (blocks / scale).astype(np.float32).astype(dtype).astype(np.float64)
    return np.moveaxis((codes * scale).reshape(v.shape), -1, axis)


WIDE = False


def mx_kscale(k):
    if not WIDE:
        return np.ones(k)
    levels = np.array([10, -10, 5, -5, 0])
    if k % 512:
        return np.exp2(np.random.permutation(np.resize(levels, k // 32))).repeat(32)
    a = np.empty((k // 512, 16))
    for p in range(k // 512):
        a[p, :8] = np.random.permutation(np.resize(levels, 8))
        for g in range(8):
            far = levels[np.abs(levels - a[p, g]) >= 10]
            a[p, g + 8] = far[np.random.randint(len(far))]
    return np.exp2(a.ravel()).repeat(32)


def f64(x):
    return np.asarray(x).astype(np.float64)


def striped(idx):
    return np.tile(np.asarray(idx).reshape(-1, 16).T, (8, 1)).astype(np.uint16)


def unstriped(offs):
    return offs[:16].T.reshape(-1).astype(np.int64)


B, N, C, D, NQ = 1, 512, 2048, 512, 128


def eight(codes):
    return np.concatenate([codes[h].reshape(-1, 16).T for h in range(8)]).astype(np.uint16)


def uneight(offs):
    return np.stack([offs[16 * h:16 * h + 16].T.reshape(-1) for h in range(8)]).astype(np.int64)


def setup_inputs():
    n = np.random.standard_normal
    s = mx_kscale(D)[:, None]
    grid = lambda x: np.round(x * 32) / 32
    return {
        "qT": (n((B, D, NQ)) * s / np.sqrt(D)).astype(np.float32),
        "cb": (grid(n((D, C))) / s).astype(np.float32),
        "norm": np.tile(np.random.randint(32, 129, N) / 64.0, (128, 1)).astype(np.float32),
        "offs": eight(np.random.randint(0, C, (8, N))),
    }


def reference(qT, cb, norm, offs):
    k = []
    for part, offs_ in enumerate((offs,)):
        codes = uneight(offs_)
        k += [f64(cb)[512 * part + 64 * h:512 * part + 64 * h + 64][:, codes[h]] for h in range(8)]
    k = np.concatenate(k) * f64(norm)[:1]
    a = mxq(f64(qT), 1, "e4m3").transpose(0, 2, 1) @ mxq(k, 0, "e4m3")
    return a

@@ -1,0 +1,132 @@
+from contextlib import ExitStack
+
+import concourse.mybir as mybir
+from concourse.masks import make_identity
+
+D, C, N, NQ = 512, 2048, 512, 128
+P = 128
+PACK = 4
+
+FLOPS = 2 * D * N * NQ
+
+F32 = mybir.dt.float32
+BF16 = mybir.dt.bfloat16
+U32 = mybir.dt.uint32
+U16 = mybir.dt.uint16
+U8 = mybir.dt.uint8
+FP8X4 = mybir.dt.float8_e4m3fn_x4
+MULT = mybir.AluOpType.mult
+
+HALF = N // 2
+CHUNK = 128
+
+
+def tile_attend_pq_att_kernel(tc, qT, cb, norm, offs, out):
+    nc = tc.nc
+    with ExitStack() as ctx:
+        keep = ctx.enter_context(tc.tile_pool(name="keep", bufs=1))
+        psum = ctx.enter_context(tc.psum_pool(name="psum", bufs=1))
+
+        offs_sb = keep.tile([P, N // 16], U16, name="offs_sb")
+        nc.sync.dma_start(offs_sb[:], offs)
+        norm_cols = keep.tile([P, PACK], F32, name="norm_cols")
+        nc.scalar.dma_start(out=norm_cols[:], in_=norm[0].rearrange("(p j) -> p j", j=PACK))
+
+        rows = cb.rearrange("(p t) c -> p t c", t=PACK)
+        windows = []
+        for t in range(PACK):
+            w = keep.tile([P, C], F32, name=f"window{t}")
+            nc.sync.dma_start(out=w[:], in_=rows[:, t, :])
+            windows.append(w)
+        q_raw = keep.tile([P, PACK, NQ], F32, name="q_raw")
+        nc.sync.dma_start(out=q_raw[:], in_=qT[0].rearrange("(p t) q -> p t q", t=PACK))
+
+        identity = keep.tile([P, P], F32, name="identity")
+        make_identity(nc, identity[:])
+        norm_ps = psum.tile([P, PACK, P], F32, name="norm_ps")
+        for j in range(PACK):
+            nc.tensor.transpose(norm_ps[:, j, :], norm_cols[:, j : j + 1].to_broadcast([P, P]), identity[:])
+        norm_sb = keep.tile([P, N], F32, name="norm_sb")
+        nc.scalar.copy(
+            out=norm_sb[:].rearrange("m (p j) -> m p j", j=PACK),
+            in_=norm_ps[:].rearrange("m j p -> m p j"),
+        )
+
+        grouped = keep.tile([P, N, PACK], BF16, name="grouped", align_bytes=64)
+        codes = keep.tile([P, N], U32, name="codes", align_bytes=64)
+        scales = keep.tile([P, N], U8, name="scales", align_bytes=64)
+        q_grouped = keep.tile([P, NQ, PACK], BF16, name="q_grouped", align_bytes=64)
+        q_codes = keep.tile([P, NQ], U32, name="q_codes", align_bytes=64)
+        q_scales = keep.tile([P, NQ], U8, name="q_scales", align_bytes=64)
+        result = keep.tile([NQ, N], F32, name="result")
+        products = [keep.tile([P, N], F32, name=f"product{t}") for t in range(PACK)]
+
+        def gather(t, a, b):
+            nc.vector.tensor_tensor(
+                products[t][:, a:b],
+                windows[t][:].indirect(offs_sb[:, a // 16 : b // 16]),
+                norm_sb[:, a:b],
+                MULT,
+            )
+
+        def place(t, a, b):
+            if a >= HALF:
+                nc.vector.tensor_copy(out=grouped[:, a:b, t], in_=products[t][:, a:b])
+            else:
+                nc.scalar.copy(out=grouped[:, a:b, t], in_=products[t][:, a:b])
+
+        def quantise(a, b):
+            nc.vector.quantize_mx(
+                out=codes[:, a:b].bitcast(FP8X4),
+                scales=scales[:, a:b],
+                in_=grouped[:, a:b, :].rearrange("p n t -> p (n t)"),
+            )
+
+        def score(bank, a, b):
+            nc.tensor.matmul_mx(
+                out=bank,
+                lhsT=q_codes[:].bitcast(FP8X4),
+                lhsT_scale=q_scales[:],
+                rhs=codes[:, a:b].bitcast(FP8X4),
+                rhs_scale=scales[:, a:b],
+                start=True,
+                stop=True,
+            )
+
+        for t in range(PACK - 1):
+            gather(t, HALF, N)
+            gather(t, 0, HALF)
+            place(t, HALF, N)
+            place(t, 0, HALF)
+
+        t = PACK - 1
+        gather(t, 0, 128)
+        gather(t, 128, 256)
+        gather(t, 256, 384)
+        gather(t, 384, 512)
+        place(t, 0, 128)
+        place(t, 128, 256)
+        nc.scalar.copy(out=q_grouped[:], in_=q_raw[:].rearrange("p t q -> p q t"))
+        quantise(0, 128)
+        place(t, 256, 384)
+        place(t, 384, 512)
+        quantise(128, 256)
+        quantise(256, 384)
+        nc.vector.quantize_mx(
+            out=q_codes[:].bitcast(FP8X4),
+            scales=q_scales[:],
+            in_=q_grouped[:].rearrange("p q t -> p (q t)"),
+        )
+        quantise(384, 512)
+
+        first = psum.tile([NQ, HALF], F32, name="first")
+        third = psum.tile([NQ, CHUNK], F32, name="third")
+        fourth = psum.tile([NQ, CHUNK], F32, name="fourth")
+        score(first[:], 0, HALF)
+        score(third[:], 256, 384)
+        score(fourth[:], 384, 512)
+        nc.scalar.copy(out=result[:, :HALF], in_=first[:])
+        nc.sync.dma_start(out=out[0, :, :HALF], in_=result[:, :HALF])
+        nc.scalar.copy(out=result[:, 256:384], in_=third[:])
+        nc.vector.tensor_copy(out=result[:, 384:512], in_=fourth[:])
+        nc.sync.dma_start(out=out[0, :, HALF:], in_=result[:, HALF:])

@@ -17,8 +17,9 @@ U8 = mybir.dt.uint8
 FP8X4 = mybir.dt.float8_e4m3fn_x4
 MULT = mybir.AluOpType.mult
 
-HALF = N // 2
 CHUNK = 128
+CHUNKS = [(a, a + CHUNK) for a in range(0, N, CHUNK)]
+VECTOR_FROM = 384
 
 
 def tile_attend_pq_att_kernel(tc, qT, cb, norm, offs, out):
@@ -33,13 +34,12 @@ def tile_attend_pq_att_kernel(tc, qT, cb, norm, offs, out):
         nc.scalar.dma_start(out=norm_cols[:], in_=norm[0].rearrange("(p j) -> p j", j=PACK))
 
         rows = cb.rearrange("(p t) c -> p t c", t=PACK)
-        windows = []
-        for t in range(PACK):
-            w = keep.tile([P, C], F32, name=f"window{t}")
-            nc.sync.dma_start(out=w[:], in_=rows[:, t, :])
-            windows.append(w)
+        windows = [keep.tile([P, C], F32, name=f"window{t}") for t in range(PACK)]
         q_raw = keep.tile([P, PACK, NQ], F32, name="q_raw")
-        nc.sync.dma_start(out=q_raw[:], in_=qT[0].rearrange("(p t) q -> p t q", t=PACK))
+        for t in range(PACK):
+            if t == 3:
+                nc.sync.dma_start(out=q_raw[:], in_=qT[0].rearrange("(p t) q -> p t q", t=PACK))
+            nc.sync.dma_start(out=windows[t][:], in_=rows[:, t, :])
 
         identity = keep.tile([P, P], F32, name="identity")
         make_identity(nc, identity[:])
@@ -55,25 +55,30 @@ def tile_attend_pq_att_kernel(tc, qT, cb, norm, offs, out):
         grouped = keep.tile([P, N, PACK], BF16, name="grouped", align_bytes=64)
         codes = keep.tile([P, N], U32, name="codes", align_bytes=64)
         scales = keep.tile([P, N], U8, name="scales", align_bytes=64)
-        q_grouped = keep.tile([P, NQ, PACK], BF16, name="q_grouped", align_bytes=64)
         q_codes = keep.tile([P, NQ], U32, name="q_codes", align_bytes=64)
         q_scales = keep.tile([P, NQ], U8, name="q_scales", align_bytes=64)
         result = keep.tile([NQ, N], F32, name="result")
-        products = [keep.tile([P, N], F32, name=f"product{t}") for t in range(PACK)]
+        s_products = [keep.tile([P, VECTOR_FROM], F32, name=f"s_product{t}") for t in range(PACK)]
+        v_products = [keep.tile([P, CHUNK], F32, name=f"v_product{t}", tag="late" if t == 2 else f"v_product{t}", align_bytes=64) for t in range(PACK)]
+
+        def product(t, a, b):
+            if a >= VECTOR_FROM:
+                return v_products[t][:]
+            return s_products[t][:, a:b]
 
         def gather(t, a, b):
             nc.vector.tensor_tensor(
-                products[t][:, a:b],
+                product(t, a, b),
                 windows[t][:].indirect(offs_sb[:, a // 16 : b // 16]),
                 norm_sb[:, a:b],
                 MULT,
             )
 
         def place(t, a, b):
-            if a >= HALF:
-                nc.vector.tensor_copy(out=grouped[:, a:b, t], in_=products[t][:, a:b])
+            if a >= VECTOR_FROM:
+                nc.vector.tensor_copy(out=grouped[:, a:b, t], in_=product(t, a, b))
             else:
-                nc.scalar.copy(out=grouped[:, a:b, t], in_=products[t][:, a:b])
+                nc.scalar.copy(out=grouped[:, a:b, t], in_=product(t, a, b))
 
         def quantise(a, b):
             nc.vector.quantize_mx(
@@ -94,39 +99,35 @@ def tile_attend_pq_att_kernel(tc, qT, cb, norm, offs, out):
             )
 
         for t in range(PACK - 1):
-            gather(t, HALF, N)
-            gather(t, 0, HALF)
-            place(t, HALF, N)
-            place(t, 0, HALF)
+            gather(t, VECTOR_FROM, N)
+            gather(t, 0, VECTOR_FROM)
+            place(t, VECTOR_FROM, N)
+            place(t, 0, VECTOR_FROM)
 
-        t = PACK - 1
-        gather(t, 0, 128)
-        gather(t, 128, 256)
-        gather(t, 256, 384)
-        gather(t, 384, 512)
-        place(t, 0, 128)
-        place(t, 128, 256)
-        nc.scalar.copy(out=q_grouped[:], in_=q_raw[:].rearrange("p t q -> p q t"))
-        quantise(0, 128)
-        place(t, 256, 384)
-        place(t, 384, 512)
-        quantise(128, 256)
-        quantise(256, 384)
+        q_grouped = keep.tile([P, NQ, PACK], BF16, name="q_grouped", tag="late", align_bytes=64)
+        nc.vector.tensor_copy(out=q_grouped[:], in_=q_raw[:].rearrange("p t q -> p q t"))
         nc.vector.quantize_mx(
             out=q_codes[:].bitcast(FP8X4),
             scales=q_scales[:],
             in_=q_grouped[:].rearrange("p q t -> p (q t)"),
         )
-        quantise(384, 512)
 
-        first = psum.tile([NQ, HALF], F32, name="first")
-        third = psum.tile([NQ, CHUNK], F32, name="third")
-        fourth = psum.tile([NQ, CHUNK], F32, name="fourth")
-        score(first[:], 0, HALF)
-        score(third[:], 256, 384)
-        score(fourth[:], 384, 512)
-        nc.scalar.copy(out=result[:, :HALF], in_=first[:])
-        nc.sync.dma_start(out=out[0, :, :HALF], in_=result[:, :HALF])
-        nc.scalar.copy(out=result[:, 256:384], in_=third[:])
-        nc.vector.tensor_copy(out=result[:, 384:512], in_=fourth[:])
-        nc.sync.dma_start(out=out[0, :, HALF:], in_=result[:, HALF:])
+        for a, b in CHUNKS:
+            gather(PACK - 1, a, b)
+        for a, b in CHUNKS[:3]:
+            place(PACK - 1, a, b)
+        quantise(*CHUNKS[0])
+        place(PACK - 1, *CHUNKS[3])
+        for a, b in CHUNKS[1:]:
+            quantise(a, b)
+
+        first = psum.tile([NQ, VECTOR_FROM], F32, name="first")
+        last = psum.tile([NQ, CHUNK], F32, name="last")
+        for a, b in CHUNKS[:3]:
+            score(first[:, a:b], a, b)
+        score(last[:], *CHUNKS[3])
+        nc.scalar.copy(out=result[:, :256], in_=first[:, :256])
+        nc.scalar.copy(out=result[:, 256:VECTOR_FROM], in_=first[:, 256:])
+        nc.sync.dma_start(out=out[0, :, :VECTOR_FROM], in_=result[:, :VECTOR_FROM])
+        nc.vector.tensor_copy(out=result[:, VECTOR_FROM:], in_=last[:])
+        nc.sync.dma_start(out=out[0, :, VECTOR_FROM:], in_=result[:, VECTOR_FROM:])

@@ -20,6 +20,7 @@ MULT = mybir.AluOpType.mult
 CHUNK = 128
 CHUNKS = [(a, a + CHUNK) for a in range(0, N, CHUNK)]
 VECTOR_FROM = 384
+SPLIT = 448
 
 
 def tile_attend_pq_att_kernel(tc, qT, cb, norm, offs, out):
@@ -63,7 +64,7 @@ def tile_attend_pq_att_kernel(tc, qT, cb, norm, offs, out):
 
         def product(t, a, b):
             if a >= VECTOR_FROM:
-                return v_products[t][:]
+                return v_products[t][:, a - VECTOR_FROM : b - VECTOR_FROM]
             return s_products[t][:, a:b]
 
         def gather(t, a, b):
@@ -75,7 +76,7 @@ def tile_attend_pq_att_kernel(tc, qT, cb, norm, offs, out):
             )
 
         def place(t, a, b):
-            if a >= VECTOR_FROM:
+            if a >= SPLIT:
                 nc.vector.tensor_copy(out=grouped[:, a:b, t], in_=product(t, a, b))
             else:
                 nc.scalar.copy(out=grouped[:, a:b, t], in_=product(t, a, b))
@@ -101,7 +102,8 @@ def tile_attend_pq_att_kernel(tc, qT, cb, norm, offs, out):
         for t in range(PACK - 1):
             gather(t, VECTOR_FROM, N)
             gather(t, 0, VECTOR_FROM)
-            place(t, VECTOR_FROM, N)
+            place(t, VECTOR_FROM, SPLIT)
+            place(t, SPLIT, N)
             place(t, 0, VECTOR_FROM)
 
         q_grouped = keep.tile([P, NQ, PACK], BF16, name="q_grouped", tag="late", align_bytes=64)
@@ -116,18 +118,22 @@ def tile_attend_pq_att_kernel(tc, qT, cb, norm, offs, out):
             gather(PACK - 1, a, b)
         for a, b in CHUNKS[:3]:
             place(PACK - 1, a, b)
+        place(PACK - 1, VECTOR_FROM, SPLIT)
         quantise(*CHUNKS[0])
-        place(PACK - 1, *CHUNKS[3])
+        place(PACK - 1, SPLIT, N)
         for a, b in CHUNKS[1:]:
             quantise(a, b)
 
-        first = psum.tile([NQ, VECTOR_FROM], F32, name="first")
+        pair = psum.tile([NQ, 2 * CHUNK], F32, name="pair")
+        third = psum.tile([NQ, CHUNK], F32, name="third")
         last = psum.tile([NQ, CHUNK], F32, name="last")
-        for a, b in CHUNKS[:3]:
-            score(first[:, a:b], a, b)
+        for a, b in CHUNKS[:2]:
+            score(pair[:, a:b], a, b)
+        nc.scalar.copy(out=result[:, :256], in_=pair[:])
+        nc.sync.dma_start(out=out[0, :, :256], in_=result[:, :256])
+        score(third[:], *CHUNKS[2])
+        nc.scalar.copy(out=result[:, 256:384], in_=third[:])
+        nc.sync.dma_start(out=out[0, :, 256:384], in_=result[:, 256:384])
         score(last[:], *CHUNKS[3])
-        nc.scalar.copy(out=result[:, :256], in_=first[:, :256])
-        nc.scalar.copy(out=result[:, 256:VECTOR_FROM], in_=first[:, 256:])
-        nc.sync.dma_start(out=out[0, :, :VECTOR_FROM], in_=result[:, :VECTOR_FROM])
-        nc.vector.tensor_copy(out=result[:, VECTOR_FROM:], in_=last[:])
-        nc.sync.dma_start(out=out[0, :, VECTOR_FROM:], in_=result[:, VECTOR_FROM:])
+        nc.vector.tensor_copy(out=result[:, 384:], in_=last[:])
+        nc.sync.dma_start(out=out[0, :, 384:], in_=result[:, 384:])

@@ -37,10 +37,11 @@ def tile_attend_pq_att_kernel(tc, qT, cb, norm, offs, out):
         rows = cb.rearrange("(p t) c -> p t c", t=PACK)
         windows = [keep.tile([P, C], F32, name=f"window{t}") for t in range(PACK)]
         q_raw = keep.tile([P, PACK, NQ], F32, name="q_raw")
-        for t in range(PACK):
-            if t == 3:
-                nc.sync.dma_start(out=q_raw[:], in_=qT[0].rearrange("(p t) q -> p t q", t=PACK))
-            nc.sync.dma_start(out=windows[t][:], in_=rows[:, t, :])
+        for t in range(PACK - 1):
+            nc.sync.dma_start(out=windows[t][:, : C // 2], in_=rows[:, t, : C // 2])
+            nc.scalar.dma_start(out=windows[t][:, C // 2 :], in_=rows[:, t, C // 2 :])
+        nc.scalar.dma_start(out=q_raw[:], in_=qT[0].rearrange("(p t) q -> p t q", t=PACK))
+        nc.sync.dma_start(out=windows[PACK - 1][:], in_=rows[:, PACK - 1, :])
 
         identity = keep.tile([P, P], F32, name="identity")
         make_identity(nc, identity[:])

@@ -40,8 +40,8 @@ def tile_attend_pq_att_kernel(tc, qT, cb, norm, offs, out):
         for t in range(PACK - 1):
             nc.sync.dma_start(out=windows[t][:, : C // 2], in_=rows[:, t, : C // 2])
             nc.scalar.dma_start(out=windows[t][:, C // 2 :], in_=rows[:, t, C // 2 :])
-        nc.scalar.dma_start(out=q_raw[:], in_=qT[0].rearrange("(p t) q -> p t q", t=PACK))
         nc.sync.dma_start(out=windows[PACK - 1][:], in_=rows[:, PACK - 1, :])
+        nc.sync.dma_start(out=q_raw[:], in_=qT[0].rearrange("(p t) q -> p t q", t=PACK))
 
         identity = keep.tile([P, P], F32, name="identity")
         make_identity(nc, identity[:])

from contextlib import ExitStack

import concourse.mybir as mybir
from concourse.masks import make_identity

D, C, N, NQ = 512, 2048, 512, 128
P = 128
PACK = 4

FLOPS = 2 * D * N * NQ

F32 = mybir.dt.float32
BF16 = mybir.dt.bfloat16
U32 = mybir.dt.uint32
U16 = mybir.dt.uint16
U8 = mybir.dt.uint8
FP8X4 = mybir.dt.float8_e4m3fn_x4
MULT = mybir.AluOpType.mult

CHUNK = 128
CHUNKS = [(a, a + CHUNK) for a in range(0, N, CHUNK)]
VECTOR_FROM = 384
SPLIT = 448


def tile_attend_pq_att_kernel(tc, qT, cb, norm, offs, out):
    nc = tc.nc
    with ExitStack() as ctx:
        keep = ctx.enter_context(tc.tile_pool(name="keep", bufs=1))
        psum = ctx.enter_context(tc.psum_pool(name="psum", bufs=1))

        offs_sb = keep.tile([P, N // 16], U16, name="offs_sb")
        nc.sync.dma_start(offs_sb[:], offs)
        norm_cols = keep.tile([P, PACK], F32, name="norm_cols")
        nc.scalar.dma_start(out=norm_cols[:], in_=norm[0].rearrange("(p j) -> p j", j=PACK))

        rows = cb.rearrange("(p t) c -> p t c", t=PACK)
        windows = [keep.tile([P, C], F32, name=f"window{t}") for t in range(PACK)]
        q_raw = keep.tile([P, PACK, NQ], F32, name="q_raw")
        for t in range(PACK - 1):
            nc.sync.dma_start(out=windows[t][:, : C // 2], in_=rows[:, t, : C // 2])
            nc.scalar.dma_start(out=windows[t][:, C // 2 :], in_=rows[:, t, C // 2 :])
        nc.sync.dma_start(out=windows[PACK - 1][:], in_=rows[:, PACK - 1, :])
        nc.sync.dma_start(out=q_raw[:], in_=qT[0].rearrange("(p t) q -> p t q", t=PACK))

        identity = keep.tile([P, P], F32, name="identity")
        make_identity(nc, identity[:])
        norm_ps = psum.tile([P, PACK, P], F32, name="norm_ps")
        for j in range(PACK):
            nc.tensor.transpose(norm_ps[:, j, :], norm_cols[:, j : j + 1].to_broadcast([P, P]), identity[:])
        norm_sb = keep.tile([P, N], F32, name="norm_sb")
        nc.scalar.copy(
            out=norm_sb[:].rearrange("m (p j) -> m p j", j=PACK),
            in_=norm_ps[:].rearrange("m j p -> m p j"),
        )

        grouped = keep.tile([P, N, PACK], BF16, name="grouped", align_bytes=64)
        codes = keep.tile([P, N], U32, name="codes", align_bytes=64)
        scales = keep.tile([P, N], U8, name="scales", align_bytes=64)
        q_codes = keep.tile([P, NQ], U32, name="q_codes", align_bytes=64)
        q_scales = keep.tile([P, NQ], U8, name="q_scales", align_bytes=64)
        result = keep.tile([NQ, N], F32, name="result")
        s_products = [keep.tile([P, VECTOR_FROM], F32, name=f"s_product{t}") for t in range(PACK)]
        v_products = [keep.tile([P, CHUNK], F32, name=f"v_product{t}", tag="late" if t == 2 else f"v_product{t}", align_bytes=64) for t in range(PACK)]

        def product(t, a, b):
            if a >= VECTOR_FROM:
                return v_products[t][:, a - VECTOR_FROM : b - VECTOR_FROM]
            return s_products[t][:, a:b]

        def gather(t, a, b):
            nc.vector.tensor_tensor(
                product(t, a, b),
                windows[t][:].indirect(offs_sb[:, a // 16 : b // 16]),
                norm_sb[:, a:b],
                MULT,
            )

        def place(t, a, b):
            if a >= SPLIT:
                nc.vector.tensor_copy(out=grouped[:, a:b, t], in_=product(t, a, b))
            else:
                nc.scalar.copy(out=grouped[:, a:b, t], in_=product(t, a, b))

        def quantise(a, b):
            nc.vector.quantize_mx(
                out=codes[:, a:b].bitcast(FP8X4),
                scales=scales[:, a:b],
                in_=grouped[:, a:b, :].rearrange("p n t -> p (n t)"),
            )

        def score(bank, a, b):
            nc.tensor.matmul_mx(
                out=bank,
                lhsT=q_codes[:].bitcast(FP8X4),
                lhsT_scale=q_scales[:],
                rhs=codes[:, a:b].bitcast(FP8X4),
                rhs_scale=scales[:, a:b],
                start=True,
                stop=True,
            )

        for t in range(PACK - 1):
            gather(t, VECTOR_FROM, N)
            gather(t, 0, VECTOR_FROM)
            place(t, VECTOR_FROM, SPLIT)
            place(t, SPLIT, N)
            place(t, 0, VECTOR_FROM)

        q_grouped = keep.tile([P, NQ, PACK], BF16, name="q_grouped", tag="late", align_bytes=64)
        nc.vector.tensor_copy(out=q_grouped[:], in_=q_raw[:].rearrange("p t q -> p q t"))
        nc.vector.quantize_mx(
            out=q_codes[:].bitcast(FP8X4),
            scales=q_scales[:],
            in_=q_grouped[:].rearrange("p q t -> p (q t)"),
        )

        for a, b in CHUNKS:
            gather(PACK - 1, a, b)
        for a, b in CHUNKS[:3]:
            place(PACK - 1, a, b)
        place(PACK - 1, VECTOR_FROM, SPLIT)
        quantise(*CHUNKS[0])
        place(PACK - 1, SPLIT, N)
        for a, b in CHUNKS[1:]:
            quantise(a, b)

        pair = psum.tile([NQ, 2 * CHUNK], F32, name="pair")
        third = psum.tile([NQ, CHUNK], F32, name="third")
        last = psum.tile([NQ, CHUNK], F32, name="last")
        for a, b in CHUNKS[:2]:
            score(pair[:, a:b], a, b)
        nc.scalar.copy(out=result[:, :256], in_=pair[:])
        nc.sync.dma_start(out=out[0, :, :256], in_=result[:, :256])
        score(third[:], *CHUNKS[2])
        nc.scalar.copy(out=result[:, 256:384], in_=third[:])
        nc.sync.dma_start(out=out[0, :, 256:384], in_=result[:, 256:384])
        score(last[:], *CHUNKS[3])
        nc.vector.tensor_copy(out=result[:, 384:], in_=last[:])
        nc.sync.dma_start(out=out[0, :, 384:], in_=result[:, 384:])
